import numpy as np
import ml_dtypes


def mxq(x, axis, fmt="e4m3"):
    dtype, down = {"e4m3": (ml_dtypes.float8_e4m3fn, 7), "e5m2": (ml_dtypes.float8_e5m2, 14)}[fmt]
    v = np.moveaxis(np.asarray(x, np.float32).astype(ml_dtypes.bfloat16).astype(np.float64), axis, -1)
    blocks = v.reshape(v.shape[:-1] + (-1, 32))
    amax = np.abs(blocks).max(-1, keepdims=True)
    byte = np.maximum(np.where(amax > 0, np.frexp(amax)[1] - 1 + 127, 0) - down, 1)
    scale = np.exp2(byte - 127.0)
    codes = (blocks / scale).astype(np.float32).astype(dtype).astype(np.float64)
    return np.moveaxis((codes * scale).reshape(v.shape), -1, axis)


WIDE = False


def mx_kscale(k):
    if not WIDE:
        return np.ones(k)
    levels = np.array([10, -10, 5, -5, 0])
    if k % 512:
        return np.exp2(np.random.permutation(np.resize(levels, k // 32))).repeat(32)
    a = np.empty((k // 512, 16))
    for p in range(k // 512):
        a[p, :8] = np.random.permutation(np.resize(levels, 8))
        for g in range(8):
            far = levels[np.abs(levels - a[p, g]) >= 10]
            a[p, g + 8] = far[np.random.randint(len(far))]
    return np.exp2(a.ravel()).repeat(32)


BF16 = ml_dtypes.bfloat16


def bf(x):
    return np.asarray(x, np.float32).astype(BF16)


def f64(x):
    return np.asarray(x).astype(np.float64)


E2M1 = np.array([0.0, 0.5, 1.0, 1.5, 2.0, 3.0, 4.0, 6.0, -0.0, -0.5, -1.0, -1.5, -2.0, -3.0, -4.0, -6.0])


def pack_weight(w, fmt):
    k, n = w.shape
    w = f64(bf(w)).reshape(k // 32, 32, n)
    amax = np.abs(w).max(1)
    if fmt == "e4m3":
        byte = np.frexp(amax)[1] - 1 + 127 - 7
    else:
        mant, ex = np.frexp(amax / 6.0)
        byte = np.where(mant > 0.5, ex, ex - 1) + 127
    byte = np.clip(np.where(amax > 0, byte, 1), 1, 254)
    scaled = (w * np.exp2(127.0 - byte)[:, None, :]).reshape(k, n).astype(np.float32)
    by_word = np.ascontiguousarray(scaled.reshape(k // 512, 128, 4, n).transpose(0, 1, 3, 2))
    if fmt == "e4m3":
        words = by_word.astype(ml_dtypes.float8_e4m3fn).view(np.uint8)
    else:
        c = by_word.astype(ml_dtypes.float4_e2m1fn).view(np.uint8) & 0xF
        words = c[..., 0::2] | (c[..., 1::2] << 4)
    return np.ascontiguousarray(words), np.ascontiguousarray(byte.astype(np.uint8).reshape(k // 512, 16, n))


def unpack_weight(words, scales, fmt):
    g, p, n, _ = words.shape
    if fmt == "e4m3":
        vals = np.ascontiguousarray(words).view(ml_dtypes.float8_e4m3fn).astype(np.float64)
    else:
        nib = np.empty((g, p, n, 4), np.uint8)
        nib[..., 0::2] = words & 0xF
        nib[..., 1::2] = words >> 4
        vals = E2M1[nib]
    vals = vals * np.repeat(np.exp2(scales.astype(np.float64) - 127.0), 8, axis=1)[..., None]
    return vals.transpose(0, 1, 3, 2).reshape(g * 512, n)
def pack4(w):
    words, scales = pack_weight(w, "e2m1")
    return words.reshape(words.shape[0], 128, -1), scales


def unpack4(words, scales):
    return unpack_weight(words.reshape(words.shape[0], 128, -1, 2), scales, "e2m1")


G, KA, KB, BA, BB = 2048, 1024, 1024, 1024, 512


def setup_inputs():
    s, u, t = mx_kscale(KA), mx_kscale(KB), mx_kscale(G)
    prim = np.random.standard_normal((KA, G)) * s[:, None] * t
    con = np.random.standard_normal((KA, BA)) / np.sqrt(KA) / G ** 0.25 / s[:, None]
    prim_words, prim_scales = pack4(prim)
    con_words, con_scales = pack4(con)
    return {"prim_words": prim_words, "prim_scales": prim_scales,
            "con_words": con_words, "con_scales": con_scales,
            "phi": bf(np.random.standard_normal((G, KB)) * u),
            "coef": bf(np.random.standard_normal((KB, BB)) / np.sqrt(KB) / u[:, None]),
            "w": bf(-np.exp(0.5 * np.random.standard_normal(G)) / G ** 0.25 / t),
            "rho": bf(np.exp(np.random.standard_normal(G)))}


def reference(prim_words, prim_scales, con_words, con_scales, phi, coef, w, rho):
    prim = unpack4(prim_words, prim_scales)
    con = unpack4(con_words, con_scales)
    chi = prim.T @ con
    psi = mxq(f64(phi), 1, "e4m3") @ mxq(f64(coef), 0, "e4m3")
    f = f64(w) * f64(rho) ** (1 / 3)
    v = psi * f[:, None]
    return mxq(chi, 0, "e4m3").T @ mxq(v, 0, "e4m3")

@@ -1,0 +1,301 @@
+from contextlib import ExitStack
+
+import concourse.mybir as mybir
+from concourse.masks import make_identity
+
+G, KA, KB, BA, BB = 2048, 1024, 1024, 1024, 512
+FLOPS = 2 * (G * KA * BA + G * KB * BB + BA * BB * G)
+
+F32 = mybir.dt.float32
+BF16 = mybir.dt.bfloat16
+I32 = mybir.dt.int32
+U32 = mybir.dt.uint32
+U8 = mybir.dt.uint8
+FP8X4 = mybir.dt.float8_e4m3fn_x4
+FP4X4 = mybir.dt.float4_e2m1fn_x4
+ALU = mybir.AluOpType
+
+P = 128
+PACK = 4
+K_PASS = 512
+GROUPS = G // K_PASS
+PASSES = 2
+M_TILES = BA // P
+BANKS = 8
+
+
+def tile_half_transformed_exchange_matrix_s12_kernel(
+    tc, prim_words, prim_scales, con_words, con_scales, phi, coef, w, rho, out
+):
+    nc = tc.nc
+    with ExitStack() as ctx:
+        keep = ctx.enter_context(tc.tile_pool(name="keep", bufs=1))
+        stage = ctx.enter_context(tc.tile_pool(name="stage", bufs=8))
+        results = ctx.enter_context(tc.tile_pool(name="results", bufs=4))
+        psum = ctx.enter_context(tc.psum_pool(name="psum", bufs=1))
+        ctx.enter_context(tc.manual_schedule())
+
+        bank_count = []
+
+        def next_bank():
+            n = len(bank_count)
+            bank_count.append(n)
+            return psum.tile([P, 512], F32, name="bank_%d" % n, tag="bank%d" % (n % BANKS))
+
+        def new_stage(label):
+            return stage.tile([P, 2048], BF16, name=label, tag="stage", align_bytes=64)
+
+        def quantize(label, src, words):
+            codes = keep.tile([P, words], U32, name=label + "_codes", align_bytes=64)
+            scales = keep.tile([P, words], U8, name=label + "_scales", align_bytes=64)
+            nc.vector.quantize_mx(out=codes[:].bitcast(FP8X4), scales=scales[:], in_=src)
+            return codes, scales
+
+        con_plane = keep.tile([P, PASSES, BA], U8, name="con_plane", align_bytes=64)
+        prim_rows_first = keep.tile([P, PASSES, 128], I32, name="prim_rows_first")
+        prim_rows_rest = keep.tile([P, PASSES, 384], I32, name="prim_rows_rest")
+        point_rows = keep.tile([P, PACK, P], F32, name="point_rows")
+        nc.vector.memset(con_plane[:].rearrange("p g n -> p (g n)").bitcast(I32), 0)
+        nc.vector.memset(prim_rows_first[:], 0)
+        nc.vector.memset(point_rows[:], 0.0)
+        nc.vector.memset(prim_rows_rest[:], 0)
+
+        ident = keep.tile([P, P], F32, name="ident")
+        make_identity(nc, ident[:])
+        third = keep.tile([P, PACK], F32, name="third")
+        nc.gpsimd.memset(third[:], 1.0)
+        nc.gpsimd.tensor_scalar(
+            out=third[:], in0=third[:], scalar1=1.0 / 3.0, scalar2=0.0, op0=ALU.mult, op1=ALU.add
+        )
+
+        point_raw = keep.tile([2 * GROUPS, K_PASS], BF16, name="point_raw")
+        nc.sync.dma_start(out=point_raw[0:GROUPS, :], in_=rho.rearrange("(j c) -> j c", j=GROUPS))
+        nc.sync.dma_start(out=point_raw[GROUPS : 2 * GROUPS, :], in_=w.rearrange("(j c) -> j c", j=GROUPS))
+
+        con_src = con_words.bitcast(I32).rearrange("g p x -> p g x")
+        prim_src = prim_words.bitcast(I32).rearrange("g p x -> p g x")
+        con_scale_src = con_scales.bitcast(I32).rearrange("g (q r) x -> r q g x", r=4)
+        prim_scale_src = prim_scales.bitcast(I32).rearrange("g (q r) x -> r q g x", r=4)
+
+        con_codes = []
+        for h in range(2):
+            con_half = keep.tile([P, PASSES, 1024], U8, name="con_codes_%d" % h, align_bytes=64)
+            con_codes.append(con_half)
+        prim_raw_first = keep.tile([P, PASSES, 256], I32, name="prim_raw_first")
+        prim_raw_rest = keep.tile([P, PASSES, 768], I32, name="prim_raw_rest")
+
+        nc.sync.dma_start(out=con_codes[0][:].bitcast(I32), in_=con_src[:, :, 0:256])
+        nc.sync.dma_start(out=prim_raw_first[:], in_=prim_src[:, :, 0:256])
+        con_plane_words = con_plane[:].bitcast(I32)
+        for r in range(4):
+            nc.sync.dma_start(out=con_plane_words[r:P:32, :, :], in_=con_scale_src[r])
+        for r in range(4):
+            nc.sync.dma_start(out=prim_rows_first[r:P:32, :, :], in_=prim_scale_src[r][:, :, 0:128])
+        nc.sync.dma_start(out=con_codes[1][:].bitcast(I32), in_=con_src[:, :, 256:512])
+
+        coef_raw = []
+        for g in range(PASSES):
+            raw = keep.tile([P, PACK, BB], BF16, name="coef_raw_%d" % g)
+            nc.sync.dma_start(
+                out=raw[:], in_=coef[g * K_PASS : (g + 1) * K_PASS, :].rearrange("(p t) n -> p t n", t=PACK)
+            )
+            coef_raw.append(raw)
+
+        phi_raw = {}
+
+        def load_phi(j):
+            for pair in range(2):
+                raw = keep.tile([P, 2, KB], BF16, name="phi_raw_%d_%d" % (j, pair))
+                row0 = j * K_PASS + pair * 256
+                nc.sync.dma_start(out=raw[:], in_=phi[row0 : row0 + 256, :].rearrange("(i c) k -> c i k", i=2))
+                phi_raw[(j, pair)] = raw
+
+        load_phi(0)
+        nc.sync.dma_start(out=prim_raw_rest[:], in_=prim_src[:, :, 256:1024])
+        for r in range(4):
+            nc.sync.dma_start(out=prim_rows_rest[r:P:32, :, :], in_=prim_scale_src[r][:, :, 128:512])
+        for j in range(1, GROUPS):
+            load_phi(j)
+
+        prim_codes = {}
+        prim_plane = {}
+
+        def sort_prim_codes(j):
+            src = prim_raw_first[:] if j == 0 else prim_raw_rest[:, :, (j - 1) * 256 : j * 256]
+            dst = keep.tile([P, PASSES, 1024], U8, name="prim_codes_%d" % j, align_bytes=64)
+            nc.vector.tensor_copy(
+                out=dst[:].bitcast(I32).rearrange("p g (t q x) -> p g t q x", t=PACK, x=4),
+                in_=src.rearrange("p g (q t x) -> p g t q x", t=PACK, x=4),
+            )
+            prim_codes[j] = dst
+
+        def sort_prim_scales(j):
+            src = prim_rows_first[:] if j == 0 else prim_rows_rest[:, :, (j - 1) * 128 : j * 128]
+            dst = keep.tile([P, PASSES, 512], U8, name="prim_plane_%d" % j, align_bytes=64)
+            nc.vector.tensor_copy(
+                out=dst[:].bitcast(I32).rearrange("p g (t q x) -> p g t q x", t=PACK, x=2),
+                in_=src.rearrange("p g (q t x) -> p g t q x", t=PACK, x=2),
+            )
+            prim_plane[j] = dst
+
+        nc.vector.tensor_copy(
+            out=point_rows[0 : 2 * GROUPS, :, :].rearrange("p t (q r) -> p t q r", r=8),
+            in_=point_raw[:].rearrange("p (q t r) -> p t q r", t=PACK, r=8),
+        )
+        point_bank = next_bank()
+        for t in range(PACK):
+            nc.tensor.transpose(point_bank[:, t * P : (t + 1) * P], point_rows[:, t, :], ident[:])
+        sort_prim_codes(0)
+        sort_prim_scales(0)
+        point_cols = keep.tile([P, 2 * GROUPS, PACK], F32, name="point_cols")
+        nc.vector.tensor_copy(
+            out=point_cols[:], in_=point_bank[:].rearrange("p (t x) -> p x t", t=PACK)[:, 0 : 2 * GROUPS, :]
+        )
+        root = keep.tile([P, GROUPS, PACK], F32, name="root")
+        factor = keep.tile([P, GROUPS, PACK], F32, name="factor")
+        for j in range(GROUPS):
+            nc.gpsimd.tensor_tensor(out=root[:, j, :], in0=point_cols[:, j, :], in1=third[:], op=ALU.pow)
+        nc.gpsimd.tensor_tensor(out=factor[:], in0=root[:], in1=point_cols[:, GROUPS:, :], op=ALU.mult)
+
+        chi_q = {}
+        phi_q = {}
+        coef_q = []
+        v_q = {}
+
+        def chi_banks(label, pairs):
+            staged = new_stage(label)
+            for slot, (j, m) in enumerate(pairs):
+                bank = next_bank()
+                h, c0 = divmod(m * P, 512)
+                for t in range(PACK):
+                    for g in range(PASSES):
+                        nc.tensor.matmul_mx(
+                            out=bank[:, t * P : (t + 1) * P],
+                            lhsT=prim_codes[j][:, g, t * 256 : (t + 1) * 256].bitcast(FP4X4),
+                            lhsT_scale=prim_plane[j][:, g, t * P : (t + 1) * P],
+                            rhs=con_codes[h][:, g, 2 * c0 : 2 * c0 + 256].bitcast(FP4X4),
+                            rhs_scale=con_plane[:, g, m * P : (m + 1) * P],
+                            start=(g == 0),
+                            stop=(g == PASSES - 1),
+                        )
+                nc.scalar.copy(
+                    out=staged[:, slot * 512 : (slot + 1) * 512].rearrange("p (c t) -> p c t", t=PACK),
+                    in_=bank[:].rearrange("p (t c) -> p c t", t=PACK),
+                )
+            return staged
+
+        def chi_quantize(label, staged, pairs, first, count):
+            codes, scales = quantize(label, staged[:, first * 512 : (first + count) * 512], count * P)
+            for s in range(count):
+                chi_q[pairs[first + s]] = (codes[:, s * P : (s + 1) * P], scales[:, s * P : (s + 1) * P])
+
+        def turn_phi(j):
+            for g in range(PASSES):
+                staged = new_stage("phi_stage_%d_%d" % (j, g))
+                words_out = staged[:].bitcast(F32).rearrange("p (t q r u) -> p q t r u", t=PACK, r=8, u=2)
+                for pair in range(2):
+                    bank = next_bank()
+                    words = phi_raw[(j, pair)][:].bitcast(F32)
+                    for u in range(2):
+                        for i in range(2):
+                            c0 = (2 * u + i) * P
+                            nc.tensor.transpose(
+                                bank[:, c0 : c0 + P], words[:, i, 256 * g + u : 256 * (g + 1) : 2], ident[:]
+                            )
+                    nc.scalar.copy(
+                        out=words_out[:, 8 * pair : 8 * pair + 8, :, :, :],
+                        in_=bank[:].rearrange("p (u q t r) -> p q t r u", u=2, t=PACK, r=8),
+                    )
+                phi_q[(j, g)] = quantize("phi_%d_%d" % (j, g), staged[:], 512)
+
+        def psi_group(j):
+            staged = new_stage("v_stage_%d" % j)
+            for n in range(BB // P):
+                bank = next_bank()
+                for t in range(PACK):
+                    for g in range(PASSES):
+                        nc.tensor.matmul_mx(
+                            out=bank[:, t * P : (t + 1) * P],
+                            lhsT=phi_q[(j, g)][0][:, t * P : (t + 1) * P].bitcast(FP8X4),
+                            lhsT_scale=phi_q[(j, g)][1][:, t * P : (t + 1) * P],
+                            rhs=coef_q[g][0][:, n * P : (n + 1) * P].bitcast(FP8X4),
+                            rhs_scale=coef_q[g][1][:, n * P : (n + 1) * P],
+                            start=(g == 0),
+                            stop=(g == PASSES - 1),
+                        )
+                nc.vector.tensor_tensor(
+                    out=staged[:, n * 512 : (n + 1) * 512].rearrange("p (c t) -> p c t", t=PACK),
+                    in0=bank[:].rearrange("p (t c) -> p c t", t=PACK),
+                    in1=factor[:, j : j + 1, :].to_broadcast([P, P, PACK]),
+                    op=ALU.mult,
+                )
+            v_q[j] = quantize("v_%d" % j, staged[:], 512)
+
+        def out_tile(m):
+            bank = next_bank()
+            for j in range(GROUPS):
+                nc.tensor.matmul_mx(
+                    out=bank[:],
+                    lhsT=chi_q[(j, m)][0].bitcast(FP8X4),
+                    lhsT_scale=chi_q[(j, m)][1],
+                    rhs=v_q[j][0][:].bitcast(FP8X4),
+                    rhs_scale=v_q[j][1][:],
+                    start=(j == 0),
+                    stop=(j == GROUPS - 1),
+                )
+            result = results.tile([P, BB], F32, name="result_%d" % m, tag="result")
+            if m % 2 == 0:
+                nc.scalar.copy(out=result[:], in_=bank[:])
+            else:
+                nc.vector.tensor_copy(out=result[:], in_=bank[:])
+            nc.sync.dma_start(out=out[m * P : (m + 1) * P, :], in_=result[:])
+
+        def chi_by_group(j, h):
+            pairs = [(j, 4 * h + s) for s in range(4)]
+            label = "chi_%d_h%d" % (j, h)
+            return label, chi_banks(label + "_stage", pairs), pairs
+
+        def chi_by_tile(m):
+            pairs = [(j, m) for j in range(1, GROUPS)]
+            staged = chi_banks("chi_m%d_stage" % m, pairs)
+            chi_quantize("chi_m%d_a" % m, staged, pairs, 0, 2)
+            chi_quantize("chi_m%d_b" % m, staged, pairs, 2, 1)
+
+        label, staged, pairs = chi_by_group(0, 0)
+        coef_stage = []
+        for g in range(PASSES):
+            grouped = new_stage("coef_stage_%d" % g)
+            nc.vector.tensor_copy(
+                out=grouped[:].rearrange("p (c i t) -> p c t i", i=4, t=PACK),
+                in_=coef_raw[g][:].rearrange("p t (c i) -> p c t i", i=4),
+            )
+            coef_stage.append(grouped)
+        for g in range(PASSES):
+            coef_q.append(quantize("coef_%d" % g, coef_stage[g][:], 512))
+        chi_quantize(label, staged, pairs, 0, 4)
+
+        label, staged, pairs = chi_by_group(0, 1)
+        sort_prim_codes(1)
+        sort_prim_scales(1)
+        chi_quantize(label, staged, pairs, 0, 4)
+
+        for j in range(1, GROUPS):
+            turn_phi(j - 1)
+            label, staged, pairs = chi_by_group(j, 0)
+            if j + 1 < GROUPS:
+                sort_prim_codes(j + 1)
+                sort_prim_scales(j + 1)
+            chi_quantize(label, staged, pairs, 0, 4)
+            psi_group(j - 1)
+        turn_phi(GROUPS - 1)
+        chi_by_tile(4)
+        psi_group(GROUPS - 1)
+        chi_by_tile(5)
+        out_tile(0)
+        out_tile(1)
+        chi_by_tile(6)
+        out_tile(2)
+        out_tile(3)
+        chi_by_tile(7)
+        for m in range(4, M_TILES):
+            out_tile(m)

@@ -14,6 +14,7 @@ U8 = mybir.dt.uint8
 FP8X4 = mybir.dt.float8_e4m3fn_x4
 FP4X4 = mybir.dt.float4_e2m1fn_x4
 ALU = mybir.AluOpType
+ACT = mybir.ActivationFunctionType
 
 P = 128
 PACK = 4
@@ -31,6 +32,8 @@ def tile_half_transformed_exchange_matrix_s12_kernel(
     with ExitStack() as ctx:
         keep = ctx.enter_context(tc.tile_pool(name="keep", bufs=1))
         stage = ctx.enter_context(tc.tile_pool(name="stage", bufs=8))
+        halves = ctx.enter_context(tc.tile_pool(name="halves", bufs=5))
+        turned = ctx.enter_context(tc.tile_pool(name="turned", bufs=4))
         results = ctx.enter_context(tc.tile_pool(name="results", bufs=4))
         psum = ctx.enter_context(tc.psum_pool(name="psum", bufs=1))
         ctx.enter_context(tc.manual_schedule())
@@ -55,22 +58,13 @@ def tile_half_transformed_exchange_matrix_s12_kernel(
         prim_rows_first = keep.tile([P, PASSES, 128], I32, name="prim_rows_first")
         prim_rows_rest = keep.tile([P, PASSES, 384], I32, name="prim_rows_rest")
         point_rows = keep.tile([P, PACK, P], F32, name="point_rows")
-        nc.vector.memset(con_plane[:].rearrange("p g n -> p (g n)").bitcast(I32), 0)
         nc.vector.memset(prim_rows_first[:], 0)
+        nc.vector.memset(con_plane[:].rearrange("p g n -> p (g n)").bitcast(I32), 0)
         nc.vector.memset(point_rows[:], 0.0)
         nc.vector.memset(prim_rows_rest[:], 0)
 
         ident = keep.tile([P, P], F32, name="ident")
         make_identity(nc, ident[:])
-        third = keep.tile([P, PACK], F32, name="third")
-        nc.gpsimd.memset(third[:], 1.0)
-        nc.gpsimd.tensor_scalar(
-            out=third[:], in0=third[:], scalar1=1.0 / 3.0, scalar2=0.0, op0=ALU.mult, op1=ALU.add
-        )
-
-        point_raw = keep.tile([2 * GROUPS, K_PASS], BF16, name="point_raw")
-        nc.sync.dma_start(out=point_raw[0:GROUPS, :], in_=rho.rearrange("(j c) -> j c", j=GROUPS))
-        nc.sync.dma_start(out=point_raw[GROUPS : 2 * GROUPS, :], in_=w.rearrange("(j c) -> j c", j=GROUPS))
 
         con_src = con_words.bitcast(I32).rearrange("g p x -> p g x")
         prim_src = prim_words.bitcast(I32).rearrange("g p x -> p g x")
@@ -81,47 +75,55 @@ def tile_half_transformed_exchange_matrix_s12_kernel(
         for h in range(2):
             con_half = keep.tile([P, PASSES, 1024], U8, name="con_codes_%d" % h, align_bytes=64)
             con_codes.append(con_half)
-        prim_raw_first = keep.tile([P, PASSES, 256], I32, name="prim_raw_first")
-        prim_raw_rest = keep.tile([P, PASSES, 768], I32, name="prim_raw_rest")
+        prim_raw = {}
+        phi_raw = {}
+        coef_raw = []
 
-        nc.sync.dma_start(out=con_codes[0][:].bitcast(I32), in_=con_src[:, :, 0:256])
-        nc.sync.dma_start(out=prim_raw_first[:], in_=prim_src[:, :, 0:256])
+        def load_prim(j, queue):
+            raw = keep.tile([P, PASSES, 256], I32, name="prim_raw_%d" % j)
+            queue.dma_start(out=raw[:], in_=prim_src[:, :, 256 * j : 256 * (j + 1)])
+            prim_raw[j] = raw
+
+        def load_phi(j, pair, queue):
+            raw = keep.tile([P, 2, KB], BF16, name="phi_raw_%d_%d" % (j, pair))
+            row0 = j * K_PASS + pair * 256
+            queue.dma_start(out=raw[:], in_=phi[row0 : row0 + 256, :].rearrange("(i c) k -> c i k", i=2))
+            phi_raw[(j, pair)] = raw
+
+        rho_rows = keep.tile([GROUPS, K_PASS], BF16, name="rho_rows")
+        w_rows = keep.tile([GROUPS, K_PASS], BF16, name="w_rows")
+        nc.sync.dma_start(out=rho_rows[:], in_=rho.rearrange("(j c) -> j c", j=GROUPS))
         con_plane_words = con_plane[:].bitcast(I32)
         for r in range(4):
-            nc.sync.dma_start(out=con_plane_words[r:P:32, :, :], in_=con_scale_src[r])
-        for r in range(4):
             nc.sync.dma_start(out=prim_rows_first[r:P:32, :, :], in_=prim_scale_src[r][:, :, 0:128])
+        load_phi(0, 0, nc.scalar)
+        load_prim(0, nc.scalar)
+        nc.scalar.dma_start(out=con_codes[0][:].bitcast(I32), in_=con_src[:, :, 0:256])
+        for r in range(4):
+            nc.sync.dma_start(out=con_plane_words[r:P:32, :, :], in_=con_scale_src[r])
+        nc.sync.dma_start(out=w_rows[:], in_=w.rearrange("(j c) -> j c", j=GROUPS))
+        load_phi(0, 1, nc.sync)
         nc.sync.dma_start(out=con_codes[1][:].bitcast(I32), in_=con_src[:, :, 256:512])
-
-        coef_raw = []
         for g in range(PASSES):
             raw = keep.tile([P, PACK, BB], BF16, name="coef_raw_%d" % g)
             nc.sync.dma_start(
                 out=raw[:], in_=coef[g * K_PASS : (g + 1) * K_PASS, :].rearrange("(p t) n -> p t n", t=PACK)
             )
             coef_raw.append(raw)
-
-        phi_raw = {}
-
-        def load_phi(j):
-            for pair in range(2):
-                raw = keep.tile([P, 2, KB], BF16, name="phi_raw_%d_%d" % (j, pair))
-                row0 = j * K_PASS + pair * 256
-                nc.sync.dma_start(out=raw[:], in_=phi[row0 : row0 + 256, :].rearrange("(i c) k -> c i k", i=2))
-                phi_raw[(j, pair)] = raw
-
-        load_phi(0)
-        nc.sync.dma_start(out=prim_raw_rest[:], in_=prim_src[:, :, 256:1024])
+        load_prim(1, nc.sync)
         for r in range(4):
             nc.sync.dma_start(out=prim_rows_rest[r:P:32, :, :], in_=prim_scale_src[r][:, :, 128:512])
         for j in range(1, GROUPS):
-            load_phi(j)
+            load_phi(j, 0, nc.sync)
+            load_phi(j, 1, nc.sync)
+            if j + 1 < GROUPS:
+                load_prim(j + 1, nc.sync)
 
         prim_codes = {}
         prim_plane = {}
 
         def sort_prim_codes(j):
-            src = prim_raw_first[:] if j == 0 else prim_raw_rest[:, :, (j - 1) * 256 : j * 256]
+            src = prim_raw[j][:]
             dst = keep.tile([P, PASSES, 1024], U8, name="prim_codes_%d" % j, align_bytes=64)
             nc.vector.tensor_copy(
                 out=dst[:].bitcast(I32).rearrange("p g (t q x) -> p g t q x", t=PACK, x=4),
@@ -138,75 +140,100 @@ def tile_half_transformed_exchange_matrix_s12_kernel(
             )
             prim_plane[j] = dst
 
-        nc.vector.tensor_copy(
-            out=point_rows[0 : 2 * GROUPS, :, :].rearrange("p t (q r) -> p t q r", r=8),
-            in_=point_raw[:].rearrange("p (q t r) -> p t q r", t=PACK, r=8),
-        )
-        point_bank = next_bank()
-        for t in range(PACK):
-            nc.tensor.transpose(point_bank[:, t * P : (t + 1) * P], point_rows[:, t, :], ident[:])
-        sort_prim_codes(0)
-        sort_prim_scales(0)
-        point_cols = keep.tile([P, 2 * GROUPS, PACK], F32, name="point_cols")
-        nc.vector.tensor_copy(
-            out=point_cols[:], in_=point_bank[:].rearrange("p (t x) -> p x t", t=PACK)[:, 0 : 2 * GROUPS, :]
-        )
-        root = keep.tile([P, GROUPS, PACK], F32, name="root")
+        log_rho = keep.tile([GROUPS, K_PASS], F32, name="log_rho")
+        root = keep.tile([GROUPS, K_PASS], F32, name="root")
         factor = keep.tile([P, GROUPS, PACK], F32, name="factor")
-        for j in range(GROUPS):
-            nc.gpsimd.tensor_tensor(out=root[:, j, :], in0=point_cols[:, j, :], in1=third[:], op=ALU.pow)
-        nc.gpsimd.tensor_tensor(out=factor[:], in0=root[:], in1=point_cols[:, GROUPS:, :], op=ALU.mult)
+        nc.scalar.activation(out=log_rho[:], in_=rho_rows[:], func=ACT.Ln)
+        nc.scalar.activation(out=root[:], in_=log_rho[:], func=ACT.Exp, scale=1.0 / 3.0)
+
+        def factor_rows():
+            nc.vector.tensor_tensor(
+                out=point_rows[0:GROUPS, :, :].rearrange("p t (q r) -> p q t r", r=8),
+                in0=root[:].rearrange("p (q t r) -> p q t r", t=PACK, r=8),
+                in1=w_rows[:].rearrange("p (q t r) -> p q t r", t=PACK, r=8),
+                op=ALU.mult,
+            )
+
+        def turn_factor():
+            bank = next_bank()
+            for t in range(PACK):
+                nc.tensor.transpose(bank[:, t * P : (t + 1) * P], point_rows[:, t, :], ident[:])
+            nc.scalar.copy(out=factor[:], in_=bank[:].rearrange("p (t x) -> p x t", t=PACK)[:, 0:GROUPS, :])
 
         chi_q = {}
         phi_q = {}
         coef_q = []
         v_q = {}
 
-        def chi_banks(label, pairs):
-            staged = new_stage(label)
-            for slot, (j, m) in enumerate(pairs):
-                bank = next_bank()
-                h, c0 = divmod(m * P, 512)
-                for t in range(PACK):
-                    for g in range(PASSES):
-                        nc.tensor.matmul_mx(
-                            out=bank[:, t * P : (t + 1) * P],
-                            lhsT=prim_codes[j][:, g, t * 256 : (t + 1) * 256].bitcast(FP4X4),
-                            lhsT_scale=prim_plane[j][:, g, t * P : (t + 1) * P],
-                            rhs=con_codes[h][:, g, 2 * c0 : 2 * c0 + 256].bitcast(FP4X4),
-                            rhs_scale=con_plane[:, g, m * P : (m + 1) * P],
-                            start=(g == 0),
-                            stop=(g == PASSES - 1),
-                        )
-                nc.scalar.copy(
-                    out=staged[:, slot * 512 : (slot + 1) * 512].rearrange("p (c t) -> p c t", t=PACK),
-                    in_=bank[:].rearrange("p (t c) -> p c t", t=PACK),
-                )
-            return staged
+        chi_halves = {}
+        chi_stage = {}
+        phi_sorted = {}
+        phi_stage = {}
+        v_stage = {}
 
-        def chi_quantize(label, staged, pairs, first, count):
-            codes, scales = quantize(label, staged[:, first * 512 : (first + count) * 512], count * P)
-            for s in range(count):
-                chi_q[pairs[first + s]] = (codes[:, s * P : (s + 1) * P], scales[:, s * P : (s + 1) * P])
-
-        def turn_phi(j):
-            for g in range(PASSES):
-                staged = new_stage("phi_stage_%d_%d" % (j, g))
-                words_out = staged[:].bitcast(F32).rearrange("p (t q r u) -> p q t r u", t=PACK, r=8, u=2)
-                for pair in range(2):
+        def chi_unit(j, h):
+            paired = halves.tile([P, 2, 2, 512], BF16, name="chi_halves_%d_%d" % (j, h), tag="halves")
+            for n in range(2):
+                for u in range(2):
                     bank = next_bank()
-                    words = phi_raw[(j, pair)][:].bitcast(F32)
-                    for u in range(2):
-                        for i in range(2):
-                            c0 = (2 * u + i) * P
-                            nc.tensor.transpose(
-                                bank[:, c0 : c0 + P], words[:, i, 256 * g + u : 256 * (g + 1) : 2], ident[:]
+                    for e in range(2):
+                        t = 2 * u + e
+                        for g in range(PASSES):
+                            nc.tensor.matmul_mx(
+                                out=bank[:, e * 256 : (e + 1) * 256],
+                                lhsT=prim_codes[j][:, g, t * 256 : (t + 1) * 256].bitcast(FP4X4),
+                                lhsT_scale=prim_plane[j][:, g, t * P : (t + 1) * P],
+                                rhs=con_codes[h][:, g, n * 512 : (n + 1) * 512].bitcast(FP4X4),
+                                rhs_scale=con_plane[:, g, h * 512 + n * 256 : h * 512 + (n + 1) * 256],
+                                start=(g == 0),
+                                stop=(g == PASSES - 1),
                             )
                     nc.scalar.copy(
-                        out=words_out[:, 8 * pair : 8 * pair + 8, :, :, :],
-                        in_=bank[:].rearrange("p (u q t r) -> p q t r u", u=2, t=PACK, r=8),
+                        out=paired[:, n, u, :].rearrange("p (c e) -> p c e", e=2),
+                        in_=bank[:].rearrange("p (e c) -> p c e", e=2),
                     )
-                phi_q[(j, g)] = quantize("phi_%d_%d" % (j, g), staged[:], 512)
+            chi_halves[(j, h)] = paired
+
+        def join_chi(j, h):
+            staged = new_stage("chi_stage_%d_%d" % (j, h))
+            nc.vector.tensor_copy(
+                out=staged[:].bitcast(F32).rearrange("p (n c u) -> p n c u", n=2, u=2),
+                in_=chi_halves[(j, h)][:].bitcast(F32).rearrange("p n u c -> p n c u"),
+            )
+            chi_stage[(j, h)] = staged
+
+        def quantize_chi(j, h):
+            codes, scales = quantize("chi_%d_%d" % (j, h), chi_stage[(j, h)][:], 512)
+            for s in range(4):
+                chi_q[(j, 4 * h + s)] = (codes[:, s * P : (s + 1) * P], scales[:, s * P : (s + 1) * P])
+
+        def sort_phi(j, pair, engine_copy=nc.vector.tensor_copy):
+            dst = turned.tile([P, 2, PASSES, 2, P], F32, name="phi_sorted_%d_%d" % (j, pair), tag="sorted")
+            engine_copy(
+                out=dst[:].rearrange("p i g u c -> p (i g) u c"),
+                in_=phi_raw[(j, pair)][:].bitcast(F32).rearrange("p i (g c u) -> p (i g) u c", g=PASSES, u=2),
+            )
+            phi_sorted[(j, pair)] = dst
+
+        def turn_phi(j, g, pair):
+            if (j, g) not in phi_stage:
+                phi_stage[(j, g)] = new_stage("phi_stage_%d_%d" % (j, g))
+            words_out = phi_stage[(j, g)][:].bitcast(F32).rearrange("p (t q r u) -> p q t r u", t=PACK, r=8, u=2)
+            bank = next_bank()
+            for u in range(2):
+                for i in range(2):
+                    c0 = (2 * u + i) * P
+                    nc.tensor.transpose(bank[:, c0 : c0 + P], phi_sorted[(j, pair)][:, i, g, u, :], ident[:])
+            nc.scalar.copy(
+                out=words_out[:, 8 * pair : 8 * pair + 8, :, :, :],
+                in_=bank[:].rearrange("p (u q t r) -> p q t r u", u=2, t=PACK, r=8),
+            )
+
+        def quantize_phi(j, g):
+            phi_q[(j, g)] = quantize("phi_%d_%d" % (j, g), phi_stage[(j, g)][:], 512)
+
+        def quantize_v(j):
+            v_q[j] = quantize("v_%d" % j, v_stage[j][:], 512)
 
         def psi_group(j):
             staged = new_stage("v_stage_%d" % j)
@@ -229,73 +256,91 @@ def tile_half_transformed_exchange_matrix_s12_kernel(
                     in1=factor[:, j : j + 1, :].to_broadcast([P, P, PACK]),
                     op=ALU.mult,
                 )
-            v_q[j] = quantize("v_%d" % j, staged[:], 512)
+            v_stage[j] = staged
 
-        def out_tile(m):
+        def out_tile(m, c0, width, engine_copy):
             bank = next_bank()
             for j in range(GROUPS):
                 nc.tensor.matmul_mx(
-                    out=bank[:],
+                    out=bank[:, 0:width],
                     lhsT=chi_q[(j, m)][0].bitcast(FP8X4),
                     lhsT_scale=chi_q[(j, m)][1],
-                    rhs=v_q[j][0][:].bitcast(FP8X4),
-                    rhs_scale=v_q[j][1][:],
+                    rhs=v_q[j][0][:, c0 : c0 + width].bitcast(FP8X4),
+                    rhs_scale=v_q[j][1][:, c0 : c0 + width],
                     start=(j == 0),
                     stop=(j == GROUPS - 1),
                 )
-            result = results.tile([P, BB], F32, name="result_%d" % m, tag="result")
-            if m % 2 == 0:
-                nc.scalar.copy(out=result[:], in_=bank[:])
-            else:
-                nc.vector.tensor_copy(out=result[:], in_=bank[:])
-            nc.sync.dma_start(out=out[m * P : (m + 1) * P, :], in_=result[:])
+            result = results.tile([P, width], F32, name="result_%d_%d" % (m, c0), tag="result")
+            engine_copy(out=result[:], in_=bank[:, 0:width])
+            nc.sync.dma_start(out=out[m * P : (m + 1) * P, c0 : c0 + width], in_=result[:])
 
-        def chi_by_group(j, h):
-            pairs = [(j, 4 * h + s) for s in range(4)]
-            label = "chi_%d_h%d" % (j, h)
-            return label, chi_banks(label + "_stage", pairs), pairs
-
-        def chi_by_tile(m):
-            pairs = [(j, m) for j in range(1, GROUPS)]
-            staged = chi_banks("chi_m%d_stage" % m, pairs)
-            chi_quantize("chi_m%d_a" % m, staged, pairs, 0, 2)
-            chi_quantize("chi_m%d_b" % m, staged, pairs, 2, 1)
-
-        label, staged, pairs = chi_by_group(0, 0)
-        coef_stage = []
-        for g in range(PASSES):
+        def group_coef(g):
             grouped = new_stage("coef_stage_%d" % g)
             nc.vector.tensor_copy(
                 out=grouped[:].rearrange("p (c i t) -> p c t i", i=4, t=PACK),
                 in_=coef_raw[g][:].rearrange("p t (c i) -> p c t i", i=4),
             )
-            coef_stage.append(grouped)
-        for g in range(PASSES):
-            coef_q.append(quantize("coef_%d" % g, coef_stage[g][:], 512))
-        chi_quantize(label, staged, pairs, 0, 4)
+            return grouped
 
-        label, staged, pairs = chi_by_group(0, 1)
+        sort_phi(0, 0)
+        sort_prim_codes(0)
+        sort_prim_scales(0)
+        for g in range(PASSES):
+            turn_phi(0, g, 0)
+        chi_unit(0, 0)
+        factor_rows()
+        sort_phi(0, 1)
+        for g in range(PASSES):
+            turn_phi(0, g, 1)
+        turn_factor()
+        chi_unit(0, 1)
+        coef_first = group_coef(0)
+        coef_second = group_coef(1)
         sort_prim_codes(1)
         sort_prim_scales(1)
-        chi_quantize(label, staged, pairs, 0, 4)
+        coef_q.append(quantize("coef_0", coef_first[:], 512))
+        quantize_phi(0, 0)
+        coef_q.append(quantize("coef_1", coef_second[:], 512))
+        quantize_phi(0, 1)
+        chi_unit(1, 0)
+        sort_phi(1, 0)
+        sort_phi(1, 1, nc.scalar.copy)
+        sort_prim_codes(2)
+        sort_prim_scales(2)
+        psi_group(0)
 
+        made = [(0, 0), (0, 1), (1, 0), (2, 0), (3, 0), (1, 1), (2, 1), (3, 1)]
         for j in range(1, GROUPS):
-            turn_phi(j - 1)
-            label, staged, pairs = chi_by_group(j, 0)
+            for g in range(PASSES):
+                for pair in range(2):
+                    turn_phi(j, g, pair)
+            join_chi(*made[j - 1])
+            quantize_phi(j, 0)
+            quantize_chi(*made[j - 1])
+            quantize_phi(j, 1)
+            chi_unit(*made[j + 2])
             if j + 1 < GROUPS:
-                sort_prim_codes(j + 1)
-                sort_prim_scales(j + 1)
-            chi_quantize(label, staged, pairs, 0, 4)
-            psi_group(j - 1)
-        turn_phi(GROUPS - 1)
-        chi_by_tile(4)
-        psi_group(GROUPS - 1)
-        chi_by_tile(5)
-        out_tile(0)
-        out_tile(1)
-        chi_by_tile(6)
-        out_tile(2)
-        out_tile(3)
-        chi_by_tile(7)
-        for m in range(4, M_TILES):
-            out_tile(m)
+                sort_phi(j + 1, 0)
+                sort_phi(j + 1, 1, nc.scalar.copy)
+            if j == 1:
+                sort_prim_codes(3)
+                sort_prim_scales(3)
+            quantize_v(j - 1)
+            psi_group(j)
+        chi_unit(*made[6])
+        join_chi(*made[3])
+        quantize_v(GROUPS - 1)
+        quantize_chi(*made[3])
+        join_chi(*made[4])
+        chi_unit(*made[7])
+        join_chi(*made[5])
+        quantize_chi(*made[4])
+        join_chi(*made[6])
+        quantize_chi(*made[5])
+        join_chi(*made[7])
+        quantize_chi(*made[6])
+        quantize_chi(*made[7])
+        for m in range(M_TILES - 1):
+            out_tile(m, 0, BB, nc.scalar.copy)
+        out_tile(M_TILES - 1, 0, 256, nc.vector.tensor_copy)
+        out_tile(M_TILES - 1, 256, 256, nc.scalar.copy)

@@ -17,12 +17,18 @@ ALU = mybir.AluOpType
 ACT = mybir.ActivationFunctionType
 
 P = 128
-PACK = 4
-K_PASS = 512
+SLOTS = 4
+K_PASS = P * SLOTS
 GROUPS = G // K_PASS
-PASSES = 2
-M_TILES = BA // P
+PASSES = KA // K_PASS
+RUN = 8
+HALF = BA // 2
+PAIR = 2 * P
+BANK = 512
 BANKS = 8
+STAGED = SLOTS * 512
+CATCH_UP = 3
+WARM_PASSES = 20
 
 
 def tile_half_transformed_exchange_matrix_s12_kernel(
@@ -31,36 +37,51 @@ def tile_half_transformed_exchange_matrix_s12_kernel(
     nc = tc.nc
     with ExitStack() as ctx:
         keep = ctx.enter_context(tc.tile_pool(name="keep", bufs=1))
-        stage = ctx.enter_context(tc.tile_pool(name="stage", bufs=8))
-        halves = ctx.enter_context(tc.tile_pool(name="halves", bufs=5))
-        turned = ctx.enter_context(tc.tile_pool(name="turned", bufs=4))
+        stage = ctx.enter_context(tc.tile_pool(name="stage", bufs=4))
+        sorted_pool = ctx.enter_context(tc.tile_pool(name="sorted_pool", bufs=4))
         results = ctx.enter_context(tc.tile_pool(name="results", bufs=4))
         psum = ctx.enter_context(tc.psum_pool(name="psum", bufs=1))
         ctx.enter_context(tc.manual_schedule())
 
-        bank_count = []
+        banks_taken = []
 
         def next_bank():
-            n = len(bank_count)
-            bank_count.append(n)
-            return psum.tile([P, 512], F32, name="bank_%d" % n, tag="bank%d" % (n % BANKS))
+            n = len(banks_taken)
+            banks_taken.append(n)
+            return psum.tile([P, BANK], F32, name="bank_%d" % n, tag="bank%d" % (n % BANKS))
 
-        def new_stage(label):
-            return stage.tile([P, 2048], BF16, name=label, tag="stage", align_bytes=64)
-
-        def quantize(label, src, words):
-            codes = keep.tile([P, words], U32, name=label + "_codes", align_bytes=64)
-            scales = keep.tile([P, words], U8, name=label + "_scales", align_bytes=64)
-            nc.vector.quantize_mx(out=codes[:].bitcast(FP8X4), scales=scales[:], in_=src)
+        def quantize(label, staged):
+            codes = keep.tile([P, 512], U32, name=label + "_codes", align_bytes=64)
+            scales = keep.tile([P, 512], U8, name=label + "_scales", align_bytes=64)
+            nc.vector.quantize_mx(out=codes[:].bitcast(FP8X4), scales=scales[:], in_=staged[:])
             return codes, scales
 
-        con_plane = keep.tile([P, PASSES, BA], U8, name="con_plane", align_bytes=64)
+        con_scale_tile = keep.tile([P, PASSES, BA], U8, name="con_scale_tile", align_bytes=64)
         prim_rows_first = keep.tile([P, PASSES, 128], I32, name="prim_rows_first")
         prim_rows_rest = keep.tile([P, PASSES, 384], I32, name="prim_rows_rest")
-        point_rows = keep.tile([P, PACK, P], F32, name="point_rows")
-        nc.vector.memset(prim_rows_first[:], 0)
-        nc.vector.memset(con_plane[:].rearrange("p g n -> p (g n)").bitcast(I32), 0)
-        nc.vector.memset(point_rows[:], 0.0)
+        factor_rows = keep.tile([P, SLOTS, P], F32, name="factor_rows")
+        nc.gpsimd.memset(prim_rows_first[:], 0)
+        nc.vector.memset(con_scale_tile[:].rearrange("p g n -> p (g n)").bitcast(I32), 0)
+
+        ones = keep.tile([P, 512], BF16, name="ones", align_bytes=64)
+        ones_codes = keep.tile([P, P], U32, name="ones_codes", align_bytes=64)
+        ones_scales = keep.tile([P, P], U8, name="ones_scales", align_bytes=64)
+        nc.gpsimd.memset(ones[:], 1.0)
+        nc.vector.quantize_mx(out=ones_codes[:].bitcast(FP8X4), scales=ones_scales[:], in_=ones[:])
+        warm_bank = next_bank()
+        for n in range(WARM_PASSES):
+            c0 = (n % SLOTS) * P
+            nc.tensor.matmul_mx(
+                out=warm_bank[:, c0 : c0 + P],
+                lhsT=ones_codes[:].bitcast(FP8X4),
+                lhsT_scale=ones_scales[:],
+                rhs=ones_codes[:].bitcast(FP8X4),
+                rhs_scale=ones_scales[:],
+                start=True,
+                stop=True,
+            )
+
+        nc.vector.memset(factor_rows[:], 0.0)
         nc.vector.memset(prim_rows_rest[:], 0)
 
         ident = keep.tile([P, P], F32, name="ident")
@@ -72,201 +93,203 @@ def tile_half_transformed_exchange_matrix_s12_kernel(
         prim_scale_src = prim_scales.bitcast(I32).rearrange("g (q r) x -> r q g x", r=4)
 
         con_codes = []
-        for h in range(2):
-            con_half = keep.tile([P, PASSES, 1024], U8, name="con_codes_%d" % h, align_bytes=64)
-            con_codes.append(con_half)
-        prim_raw = {}
+        prim_raw = []
         phi_raw = {}
         coef_raw = []
+
+        def load_con(h, queue):
+            half = keep.tile([P, PASSES, 2 * HALF], U8, name="con_codes_%d" % h, align_bytes=64)
+            queue.dma_start(out=half[:].bitcast(I32), in_=con_src[:, :, 256 * h : 256 * (h + 1)])
+            con_codes.append(half)
 
         def load_prim(j, queue):
             raw = keep.tile([P, PASSES, 256], I32, name="prim_raw_%d" % j)
             queue.dma_start(out=raw[:], in_=prim_src[:, :, 256 * j : 256 * (j + 1)])
-            prim_raw[j] = raw
+            prim_raw.append(raw)
 
-        def load_phi(j, pair, queue):
-            raw = keep.tile([P, 2, KB], BF16, name="phi_raw_%d_%d" % (j, pair))
-            row0 = j * K_PASS + pair * 256
-            queue.dma_start(out=raw[:], in_=phi[row0 : row0 + 256, :].rearrange("(i c) k -> c i k", i=2))
-            phi_raw[(j, pair)] = raw
+        def load_scale_rows(dst, src):
+            for r in range(4):
+                nc.sync.dma_start(out=dst[r:P:32, :, :], in_=src[r])
+
+        def load_phi(j):
+            for pair in range(2):
+                raw = keep.tile([P, 2, KB], BF16, name="phi_raw_%d_%d" % (j, pair))
+                row0 = j * K_PASS + pair * PAIR
+                nc.sync.dma_start(out=raw[:], in_=phi[row0 : row0 + PAIR, :].rearrange("(i c) k -> c i k", i=2))
+                phi_raw[(j, pair)] = raw
+
+        def load_coef(g):
+            raw = keep.tile([P, SLOTS, BB], BF16, name="coef_raw_%d" % g)
+            rows = coef[g * K_PASS : (g + 1) * K_PASS, :]
+            nc.sync.dma_start(out=raw[:], in_=rows.rearrange("(p t) n -> p t n", t=SLOTS))
+            coef_raw.append(raw)
 
         rho_rows = keep.tile([GROUPS, K_PASS], BF16, name="rho_rows")
         w_rows = keep.tile([GROUPS, K_PASS], BF16, name="w_rows")
         nc.sync.dma_start(out=rho_rows[:], in_=rho.rearrange("(j c) -> j c", j=GROUPS))
-        con_plane_words = con_plane[:].bitcast(I32)
-        for r in range(4):
-            nc.sync.dma_start(out=prim_rows_first[r:P:32, :, :], in_=prim_scale_src[r][:, :, 0:128])
-        load_phi(0, 0, nc.scalar)
+        load_scale_rows(prim_rows_first, prim_scale_src[:, :, :, 0:128])
         load_prim(0, nc.scalar)
-        nc.scalar.dma_start(out=con_codes[0][:].bitcast(I32), in_=con_src[:, :, 0:256])
-        for r in range(4):
-            nc.sync.dma_start(out=con_plane_words[r:P:32, :, :], in_=con_scale_src[r])
+        load_con(0, nc.scalar)
+        load_scale_rows(con_scale_tile[:].bitcast(I32), con_scale_src)
         nc.sync.dma_start(out=w_rows[:], in_=w.rearrange("(j c) -> j c", j=GROUPS))
-        load_phi(0, 1, nc.sync)
-        nc.sync.dma_start(out=con_codes[1][:].bitcast(I32), in_=con_src[:, :, 256:512])
-        for g in range(PASSES):
-            raw = keep.tile([P, PACK, BB], BF16, name="coef_raw_%d" % g)
-            nc.sync.dma_start(
-                out=raw[:], in_=coef[g * K_PASS : (g + 1) * K_PASS, :].rearrange("(p t) n -> p t n", t=PACK)
-            )
-            coef_raw.append(raw)
+        load_con(1, nc.sync)
         load_prim(1, nc.sync)
-        for r in range(4):
-            nc.sync.dma_start(out=prim_rows_rest[r:P:32, :, :], in_=prim_scale_src[r][:, :, 128:512])
+        load_scale_rows(prim_rows_rest, prim_scale_src[:, :, :, 128:512])
+        load_phi(0)
+        for g in range(PASSES):
+            load_coef(g)
         for j in range(1, GROUPS):
-            load_phi(j, 0, nc.sync)
-            load_phi(j, 1, nc.sync)
             if j + 1 < GROUPS:
                 load_prim(j + 1, nc.sync)
+            load_phi(j)
 
-        prim_codes = {}
-        prim_plane = {}
+        prim_sorted = []
 
-        def sort_prim_codes(j):
-            src = prim_raw[j][:]
-            dst = keep.tile([P, PASSES, 1024], U8, name="prim_codes_%d" % j, align_bytes=64)
+        def sort_prim(j):
+            codes = keep.tile([P, PASSES, 2 * K_PASS], U8, name="prim_codes_%d" % j, align_bytes=64)
             nc.vector.tensor_copy(
-                out=dst[:].bitcast(I32).rearrange("p g (t q x) -> p g t q x", t=PACK, x=4),
-                in_=src.rearrange("p g (q t x) -> p g t q x", t=PACK, x=4),
+                out=codes[:].bitcast(I32).rearrange("p g (t q x) -> p g t q x", t=SLOTS, x=RUN // 2),
+                in_=prim_raw[j][:].rearrange("p g (q t x) -> p g t q x", t=SLOTS, x=RUN // 2),
             )
-            prim_codes[j] = dst
-
-        def sort_prim_scales(j):
-            src = prim_rows_first[:] if j == 0 else prim_rows_rest[:, :, (j - 1) * 128 : j * 128]
-            dst = keep.tile([P, PASSES, 512], U8, name="prim_plane_%d" % j, align_bytes=64)
+            rows = prim_rows_first[:] if j == 0 else prim_rows_rest[:, :, (j - 1) * 128 : j * 128]
+            scales = keep.tile([P, PASSES, K_PASS], U8, name="prim_scales_%d" % j, align_bytes=64)
             nc.vector.tensor_copy(
-                out=dst[:].bitcast(I32).rearrange("p g (t q x) -> p g t q x", t=PACK, x=2),
-                in_=src.rearrange("p g (q t x) -> p g t q x", t=PACK, x=2),
+                out=scales[:].bitcast(I32).rearrange("p g (t q x) -> p g t q x", t=SLOTS, x=RUN // 4),
+                in_=rows.rearrange("p g (q t x) -> p g t q x", t=SLOTS, x=RUN // 4),
             )
-            prim_plane[j] = dst
+            prim_sorted.append((codes, scales))
 
         log_rho = keep.tile([GROUPS, K_PASS], F32, name="log_rho")
         root = keep.tile([GROUPS, K_PASS], F32, name="root")
-        factor = keep.tile([P, GROUPS, PACK], F32, name="factor")
+        factor = keep.tile([P, GROUPS, SLOTS], F32, name="factor")
         nc.scalar.activation(out=log_rho[:], in_=rho_rows[:], func=ACT.Ln)
         nc.scalar.activation(out=root[:], in_=log_rho[:], func=ACT.Exp, scale=1.0 / 3.0)
 
-        def factor_rows():
+        def make_factor_rows():
             nc.vector.tensor_tensor(
-                out=point_rows[0:GROUPS, :, :].rearrange("p t (q r) -> p q t r", r=8),
-                in0=root[:].rearrange("p (q t r) -> p q t r", t=PACK, r=8),
-                in1=w_rows[:].rearrange("p (q t r) -> p q t r", t=PACK, r=8),
+                out=factor_rows[0:GROUPS, :, :].rearrange("p t (q r) -> p q t r", r=RUN),
+                in0=root[:].rearrange("p (q t r) -> p q t r", t=SLOTS, r=RUN),
+                in1=w_rows[:].rearrange("p (q t r) -> p q t r", t=SLOTS, r=RUN),
                 op=ALU.mult,
             )
 
         def turn_factor():
             bank = next_bank()
-            for t in range(PACK):
-                nc.tensor.transpose(bank[:, t * P : (t + 1) * P], point_rows[:, t, :], ident[:])
-            nc.scalar.copy(out=factor[:], in_=bank[:].rearrange("p (t x) -> p x t", t=PACK)[:, 0:GROUPS, :])
+            for t in range(SLOTS):
+                nc.tensor.transpose(bank[:, t * P : (t + 1) * P], factor_rows[:, t, :], ident[:])
+            nc.scalar.copy(out=factor[:], in_=bank[:].rearrange("p (t j) -> p j t", t=SLOTS)[:, 0:GROUPS, :])
 
-        chi_q = {}
-        phi_q = {}
-        coef_q = []
-        v_q = {}
-
-        chi_halves = {}
-        chi_stage = {}
+        chi_staged = {}
+        chi_mx = {}
+        coef_staged = []
+        coef_mx = []
         phi_sorted = {}
-        phi_stage = {}
-        v_stage = {}
+        phi_staged = {}
+        phi_mx = {}
+        v_staged = {}
+        v_mx = {}
 
-        def chi_unit(j, h):
-            paired = halves.tile([P, 2, 2, 512], BF16, name="chi_halves_%d_%d" % (j, h), tag="halves")
-            for n in range(2):
-                for u in range(2):
-                    bank = next_bank()
-                    for e in range(2):
-                        t = 2 * u + e
-                        for g in range(PASSES):
-                            nc.tensor.matmul_mx(
-                                out=bank[:, e * 256 : (e + 1) * 256],
-                                lhsT=prim_codes[j][:, g, t * 256 : (t + 1) * 256].bitcast(FP4X4),
-                                lhsT_scale=prim_plane[j][:, g, t * P : (t + 1) * P],
-                                rhs=con_codes[h][:, g, n * 512 : (n + 1) * 512].bitcast(FP4X4),
-                                rhs_scale=con_plane[:, g, h * 512 + n * 256 : h * 512 + (n + 1) * 256],
-                                start=(g == 0),
-                                stop=(g == PASSES - 1),
-                            )
-                    nc.scalar.copy(
-                        out=paired[:, n, u, :].rearrange("p (c e) -> p c e", e=2),
-                        in_=bank[:].rearrange("p (e c) -> p c e", e=2),
-                    )
-            chi_halves[(j, h)] = paired
-
-        def join_chi(j, h):
-            staged = new_stage("chi_stage_%d_%d" % (j, h))
-            nc.vector.tensor_copy(
-                out=staged[:].bitcast(F32).rearrange("p (n c u) -> p n c u", n=2, u=2),
-                in_=chi_halves[(j, h)][:].bitcast(F32).rearrange("p n u c -> p n c u"),
-            )
-            chi_stage[(j, h)] = staged
-
-        def quantize_chi(j, h):
-            codes, scales = quantize("chi_%d_%d" % (j, h), chi_stage[(j, h)][:], 512)
-            for s in range(4):
-                chi_q[(j, 4 * h + s)] = (codes[:, s * P : (s + 1) * P], scales[:, s * P : (s + 1) * P])
-
-        def sort_phi(j, pair, engine_copy=nc.vector.tensor_copy):
-            dst = turned.tile([P, 2, PASSES, 2, P], F32, name="phi_sorted_%d_%d" % (j, pair), tag="sorted")
-            engine_copy(
-                out=dst[:].rearrange("p i g u c -> p (i g) u c"),
-                in_=phi_raw[(j, pair)][:].bitcast(F32).rearrange("p i (g c u) -> p (i g) u c", g=PASSES, u=2),
-            )
-            phi_sorted[(j, pair)] = dst
-
-        def turn_phi(j, g, pair):
-            if (j, g) not in phi_stage:
-                phi_stage[(j, g)] = new_stage("phi_stage_%d_%d" % (j, g))
-            words_out = phi_stage[(j, g)][:].bitcast(F32).rearrange("p (t q r u) -> p q t r u", t=PACK, r=8, u=2)
-            bank = next_bank()
-            for u in range(2):
-                for i in range(2):
-                    c0 = (2 * u + i) * P
-                    nc.tensor.transpose(bank[:, c0 : c0 + P], phi_sorted[(j, pair)][:, i, g, u, :], ident[:])
-            nc.scalar.copy(
-                out=words_out[:, 8 * pair : 8 * pair + 8, :, :, :],
-                in_=bank[:].rearrange("p (u q t r) -> p q t r u", u=2, t=PACK, r=8),
-            )
-
-        def quantize_phi(j, g):
-            phi_q[(j, g)] = quantize("phi_%d_%d" % (j, g), phi_stage[(j, g)][:], 512)
-
-        def quantize_v(j):
-            v_q[j] = quantize("v_%d" % j, v_stage[j][:], 512)
-
-        def psi_group(j):
-            staged = new_stage("v_stage_%d" % j)
-            for n in range(BB // P):
+        def chi_half(j, h):
+            codes, scales = prim_sorted[j]
+            staged = keep.tile([P, STAGED], BF16, name="chi_staged_%d_%d" % (j, h), align_bytes=64)
+            for n in range(HALF // P):
                 bank = next_bank()
-                for t in range(PACK):
+                col0 = h * HALF + n * P
+                for t in range(SLOTS):
                     for g in range(PASSES):
                         nc.tensor.matmul_mx(
                             out=bank[:, t * P : (t + 1) * P],
-                            lhsT=phi_q[(j, g)][0][:, t * P : (t + 1) * P].bitcast(FP8X4),
-                            lhsT_scale=phi_q[(j, g)][1][:, t * P : (t + 1) * P],
-                            rhs=coef_q[g][0][:, n * P : (n + 1) * P].bitcast(FP8X4),
-                            rhs_scale=coef_q[g][1][:, n * P : (n + 1) * P],
+                            lhsT=codes[:, g, 2 * t * P : 2 * (t + 1) * P].bitcast(FP4X4),
+                            lhsT_scale=scales[:, g, t * P : (t + 1) * P],
+                            rhs=con_codes[h][:, g, 2 * n * P : 2 * (n + 1) * P].bitcast(FP4X4),
+                            rhs_scale=con_scale_tile[:, g, col0 : col0 + P],
+                            start=(g == 0),
+                            stop=(g == PASSES - 1),
+                        )
+                nc.scalar.copy(
+                    out=staged[:, n * BANK : (n + 1) * BANK].rearrange("p (c t) -> p c t", t=SLOTS),
+                    in_=bank[:].rearrange("p (t c) -> p c t", t=SLOTS),
+                )
+            chi_staged[(j, h)] = staged
+
+        def quantize_chi(j, h):
+            chi_mx[(j, h)] = quantize("chi_%d_%d" % (j, h), chi_staged[(j, h)])
+
+        def stage_coef(g):
+            staged = stage.tile([P, STAGED], BF16, name="coef_staged_%d" % g, tag="staged", align_bytes=64)
+            nc.vector.tensor_copy(
+                out=staged[:].rearrange("p (c i t) -> p c t i", i=4, t=SLOTS),
+                in_=coef_raw[g][:].rearrange("p t (c i) -> p c t i", i=4),
+            )
+            coef_staged.append(staged)
+
+        def quantize_coef(g):
+            coef_mx.append(quantize("coef_%d" % g, coef_staged[g]))
+
+        def sort_phi(j, pair, engine_copy):
+            parted = sorted_pool.tile([P, 2, PASSES, 2, P], F32, name="phi_sorted_%d_%d" % (j, pair), tag="sorted")
+            engine_copy(
+                out=parted[:].rearrange("p i g u c -> p (i g) u c"),
+                in_=phi_raw[(j, pair)][:].bitcast(F32).rearrange("p i (g c u) -> p (i g) u c", g=PASSES, u=2),
+            )
+            phi_sorted[(j, pair)] = parted
+
+        def turn_phi(j):
+            for g in range(PASSES):
+                staged = stage.tile([P, STAGED], BF16, name="phi_staged_%d_%d" % (j, g), tag="staged", align_bytes=64)
+                words = staged[:].bitcast(F32).rearrange("p (t q r u) -> p q t r u", t=SLOTS, r=RUN, u=2)
+                for pair in range(2):
+                    bank = next_bank()
+                    for u in range(2):
+                        for i in range(2):
+                            c0 = (2 * u + i) * P
+                            nc.tensor.transpose(bank[:, c0 : c0 + P], phi_sorted[(j, pair)][:, i, g, u, :], ident[:])
+                    nc.scalar.copy(
+                        out=words[:, 8 * pair : 8 * (pair + 1), :, :, :],
+                        in_=bank[:].rearrange("p (u q t r) -> p q t r u", u=2, t=SLOTS, r=RUN),
+                    )
+                phi_staged[(j, g)] = staged
+
+        def quantize_phi(j):
+            for g in range(PASSES):
+                phi_mx[(j, g)] = quantize("phi_%d_%d" % (j, g), phi_staged[(j, g)])
+
+        def psi_group(j):
+            staged = keep.tile([P, STAGED], BF16, name="v_staged_%d" % j, align_bytes=64)
+            for n in range(BB // P):
+                bank = next_bank()
+                for t in range(SLOTS):
+                    for g in range(PASSES):
+                        nc.tensor.matmul_mx(
+                            out=bank[:, t * P : (t + 1) * P],
+                            lhsT=phi_mx[(j, g)][0][:, t * P : (t + 1) * P].bitcast(FP8X4),
+                            lhsT_scale=phi_mx[(j, g)][1][:, t * P : (t + 1) * P],
+                            rhs=coef_mx[g][0][:, n * P : (n + 1) * P].bitcast(FP8X4),
+                            rhs_scale=coef_mx[g][1][:, n * P : (n + 1) * P],
                             start=(g == 0),
                             stop=(g == PASSES - 1),
                         )
                 nc.vector.tensor_tensor(
-                    out=staged[:, n * 512 : (n + 1) * 512].rearrange("p (c t) -> p c t", t=PACK),
-                    in0=bank[:].rearrange("p (t c) -> p c t", t=PACK),
-                    in1=factor[:, j : j + 1, :].to_broadcast([P, P, PACK]),
+                    out=staged[:, n * BANK : (n + 1) * BANK].rearrange("p (c t) -> p c t", t=SLOTS),
+                    in0=bank[:].rearrange("p (t c) -> p c t", t=SLOTS),
+                    in1=factor[:, j : j + 1, :].to_broadcast([P, P, SLOTS]),
                     op=ALU.mult,
                 )
-            v_stage[j] = staged
+            v_staged[j] = staged
+
+        def quantize_v(j):
+            v_mx[j] = quantize("v_%d" % j, v_staged[j])
 
         def out_tile(m, c0, width, engine_copy):
+            h, n = divmod(m, HALF // P)
             bank = next_bank()
             for j in range(GROUPS):
                 nc.tensor.matmul_mx(
                     out=bank[:, 0:width],
-                    lhsT=chi_q[(j, m)][0].bitcast(FP8X4),
-                    lhsT_scale=chi_q[(j, m)][1],
-                    rhs=v_q[j][0][:, c0 : c0 + width].bitcast(FP8X4),
-                    rhs_scale=v_q[j][1][:, c0 : c0 + width],
+                    lhsT=chi_mx[(j, h)][0][:, n * P : (n + 1) * P].bitcast(FP8X4),
+                    lhsT_scale=chi_mx[(j, h)][1][:, n * P : (n + 1) * P],
+                    rhs=v_mx[j][0][:, c0 : c0 + width].bitcast(FP8X4),
+                    rhs_scale=v_mx[j][1][:, c0 : c0 + width],
                     start=(j == 0),
                     stop=(j == GROUPS - 1),
                 )
@@ -274,73 +297,54 @@ def tile_half_transformed_exchange_matrix_s12_kernel(
             engine_copy(out=result[:], in_=bank[:, 0:width])
             nc.sync.dma_start(out=out[m * P : (m + 1) * P, c0 : c0 + width], in_=result[:])
 
-        def group_coef(g):
-            grouped = new_stage("coef_stage_%d" % g)
-            nc.vector.tensor_copy(
-                out=grouped[:].rearrange("p (c i t) -> p c t i", i=4, t=PACK),
-                in_=coef_raw[g][:].rearrange("p t (c i) -> p c t i", i=4),
-            )
-            return grouped
-
-        sort_phi(0, 0)
-        sort_prim_codes(0)
-        sort_prim_scales(0)
-        for g in range(PASSES):
-            turn_phi(0, g, 0)
-        chi_unit(0, 0)
-        factor_rows()
-        sort_phi(0, 1)
-        for g in range(PASSES):
-            turn_phi(0, g, 1)
+        sort_prim(0)
+        chi_half(0, 0)
+        make_factor_rows()
+        sort_prim(1)
+        chi_half(0, 1)
+        quantize_chi(0, 0)
+        sort_phi(0, 0, nc.vector.tensor_copy)
+        sort_phi(0, 1, nc.vector.tensor_copy)
+        chi_half(1, 0)
+        stage_coef(0)
+        stage_coef(1)
+        sort_prim(2)
+        turn_phi(0)
         turn_factor()
-        chi_unit(0, 1)
-        coef_first = group_coef(0)
-        coef_second = group_coef(1)
-        sort_prim_codes(1)
-        sort_prim_scales(1)
-        coef_q.append(quantize("coef_0", coef_first[:], 512))
-        quantize_phi(0, 0)
-        coef_q.append(quantize("coef_1", coef_second[:], 512))
-        quantize_phi(0, 1)
-        chi_unit(1, 0)
-        sort_phi(1, 0)
-        sort_phi(1, 1, nc.scalar.copy)
-        sort_prim_codes(2)
-        sort_prim_scales(2)
-        psi_group(0)
+        quantize_coef(0)
+        quantize_coef(1)
+        chi_half(2, 0)
+        sort_phi(1, 0, nc.vector.tensor_copy)
+        sort_phi(1, 1, nc.vector.tensor_copy)
+        quantize_phi(0)
+        sort_prim(3)
 
-        made = [(0, 0), (0, 1), (1, 0), (2, 0), (3, 0), (1, 1), (2, 1), (3, 1)]
-        for j in range(1, GROUPS):
-            for g in range(PASSES):
-                for pair in range(2):
-                    turn_phi(j, g, pair)
-            join_chi(*made[j - 1])
-            quantize_phi(j, 0)
-            quantize_chi(*made[j - 1])
-            quantize_phi(j, 1)
-            chi_unit(*made[j + 2])
+        waiting = [(quantize_chi, (j, 0)) for j in range(1, GROUPS)]
+        waiting.extend([(quantize_v, (j,)) for j in range(GROUPS)])
+        waiting.extend([(quantize_chi, (j, 1)) for j in range(GROUPS)])
+        chi_to_make = [(GROUPS - 1, 0)] + [(j, 1) for j in range(1, GROUPS)]
+
+        def catch_up(count):
+            for job, args in waiting[0:count]:
+                waiting.remove((job, args))
+                job(*args)
+
+        for j in range(GROUPS):
             if j + 1 < GROUPS:
-                sort_phi(j + 1, 0)
-                sort_phi(j + 1, 1, nc.scalar.copy)
-            if j == 1:
-                sort_prim_codes(3)
-                sort_prim_scales(3)
-            quantize_v(j - 1)
+                turn_phi(j + 1)
+            if j + 2 < GROUPS:
+                sort_phi(j + 2, 1, nc.scalar.copy)
+                sort_phi(j + 2, 0, nc.vector.tensor_copy)
+            else:
+                catch_up(CATCH_UP)
             psi_group(j)
-        chi_unit(*made[6])
-        join_chi(*made[3])
-        quantize_v(GROUPS - 1)
-        quantize_chi(*made[3])
-        join_chi(*made[4])
-        chi_unit(*made[7])
-        join_chi(*made[5])
-        quantize_chi(*made[4])
-        join_chi(*made[6])
-        quantize_chi(*made[5])
-        join_chi(*made[7])
-        quantize_chi(*made[6])
-        quantize_chi(*made[7])
-        for m in range(M_TILES - 1):
+            if j + 1 < GROUPS:
+                quantize_phi(j + 1)
+            chi_half(*chi_to_make[j])
+        catch_up(len(waiting))
+
+        last = BA // P - 1
+        for m in range(last):
             out_tile(m, 0, BB, nc.scalar.copy)
-        out_tile(M_TILES - 1, 0, 256, nc.vector.tensor_copy)
-        out_tile(M_TILES - 1, 256, 256, nc.scalar.copy)
+        out_tile(last, 0, BB // 2, nc.vector.tensor_copy)
+        out_tile(last, BB // 2, BB // 2, nc.scalar.copy)

@@ -23,6 +23,7 @@ GROUPS = G // K_PASS
 PASSES = KA // K_PASS
 RUN = 8
 HALF = BA // 2
+WIDE = 256
 PAIR = 2 * P
 BANK = 512
 BANKS = 8
@@ -39,6 +40,7 @@ def tile_half_transformed_exchange_matrix_s12_kernel(
         keep = ctx.enter_context(tc.tile_pool(name="keep", bufs=1))
         stage = ctx.enter_context(tc.tile_pool(name="stage", bufs=4))
         sorted_pool = ctx.enter_context(tc.tile_pool(name="sorted_pool", bufs=4))
+        paired_pool = ctx.enter_context(tc.tile_pool(name="paired_pool", bufs=2))
         results = ctx.enter_context(tc.tile_pool(name="results", bufs=4))
         psum = ctx.enter_context(tc.psum_pool(name="psum", bufs=1))
         ctx.enter_context(tc.manual_schedule())
@@ -132,12 +134,12 @@ def tile_half_transformed_exchange_matrix_s12_kernel(
         load_con(0, nc.scalar)
         load_scale_rows(con_scale_tile[:].bitcast(I32), con_scale_src)
         nc.sync.dma_start(out=w_rows[:], in_=w.rearrange("(j c) -> j c", j=GROUPS))
+        load_coef(0)
         load_con(1, nc.sync)
         load_prim(1, nc.sync)
         load_scale_rows(prim_rows_rest, prim_scale_src[:, :, :, 128:512])
         load_phi(0)
-        for g in range(PASSES):
-            load_coef(g)
+        load_coef(1)
         for j in range(1, GROUPS):
             if j + 1 < GROUPS:
                 load_prim(j + 1, nc.sync)
@@ -180,6 +182,7 @@ def tile_half_transformed_exchange_matrix_s12_kernel(
             nc.scalar.copy(out=factor[:], in_=bank[:].rearrange("p (t j) -> p j t", t=SLOTS)[:, 0:GROUPS, :])
 
         chi_staged = {}
+        chi_paired = {}
         chi_mx = {}
         coef_staged = []
         coef_mx = []
@@ -189,20 +192,19 @@ def tile_half_transformed_exchange_matrix_s12_kernel(
         v_staged = {}
         v_mx = {}
 
-        def chi_half(j, h):
+        def chi_narrow(j):
             codes, scales = prim_sorted[j]
-            staged = keep.tile([P, STAGED], BF16, name="chi_staged_%d_%d" % (j, h), align_bytes=64)
+            staged = keep.tile([P, STAGED], BF16, name="chi_staged_%d_0" % j, align_bytes=64)
             for n in range(HALF // P):
                 bank = next_bank()
-                col0 = h * HALF + n * P
                 for t in range(SLOTS):
                     for g in range(PASSES):
                         nc.tensor.matmul_mx(
                             out=bank[:, t * P : (t + 1) * P],
                             lhsT=codes[:, g, 2 * t * P : 2 * (t + 1) * P].bitcast(FP4X4),
                             lhsT_scale=scales[:, g, t * P : (t + 1) * P],
-                            rhs=con_codes[h][:, g, 2 * n * P : 2 * (n + 1) * P].bitcast(FP4X4),
-                            rhs_scale=con_scale_tile[:, g, col0 : col0 + P],
+                            rhs=con_codes[0][:, g, 2 * n * P : 2 * (n + 1) * P].bitcast(FP4X4),
+                            rhs_scale=con_scale_tile[:, g, n * P : (n + 1) * P],
                             start=(g == 0),
                             stop=(g == PASSES - 1),
                         )
@@ -210,7 +212,40 @@ def tile_half_transformed_exchange_matrix_s12_kernel(
                     out=staged[:, n * BANK : (n + 1) * BANK].rearrange("p (c t) -> p c t", t=SLOTS),
                     in_=bank[:].rearrange("p (t c) -> p c t", t=SLOTS),
                 )
-            chi_staged[(j, h)] = staged
+            chi_staged[(j, 0)] = staged
+
+        def chi_wide(j):
+            codes, scales = prim_sorted[j]
+            paired = paired_pool.tile([P, HALF // WIDE, 2, BANK], BF16, name="chi_paired_%d" % j, tag="paired")
+            for n in range(HALF // WIDE):
+                col0 = HALF + n * WIDE
+                for u in range(2):
+                    bank = next_bank()
+                    for e in range(2):
+                        t = 2 * u + e
+                        for g in range(PASSES):
+                            nc.tensor.matmul_mx(
+                                out=bank[:, e * WIDE : (e + 1) * WIDE],
+                                lhsT=codes[:, g, 2 * t * P : 2 * (t + 1) * P].bitcast(FP4X4),
+                                lhsT_scale=scales[:, g, t * P : (t + 1) * P],
+                                rhs=con_codes[1][:, g, 2 * n * WIDE : 2 * (n + 1) * WIDE].bitcast(FP4X4),
+                                rhs_scale=con_scale_tile[:, g, col0 : col0 + WIDE],
+                                start=(g == 0),
+                                stop=(g == PASSES - 1),
+                            )
+                    nc.scalar.copy(
+                        out=paired[:, n, u, :].rearrange("p (c e) -> p c e", e=2),
+                        in_=bank[:].rearrange("p (e c) -> p c e", e=2),
+                    )
+            chi_paired[j] = paired
+
+        def join_chi(j, engine_copy):
+            staged = keep.tile([P, STAGED], BF16, name="chi_staged_%d_1" % j, align_bytes=64)
+            engine_copy(
+                out=staged[:].bitcast(F32).rearrange("p (n c u) -> p n c u", n=HALF // WIDE, u=2),
+                in_=chi_paired[j][:].bitcast(F32).rearrange("p n u c -> p n c u"),
+            )
+            chi_staged[(j, 1)] = staged
 
         def quantize_chi(j, h):
             chi_mx[(j, h)] = quantize("chi_%d_%d" % (j, h), chi_staged[(j, h)])
@@ -226,9 +261,9 @@ def tile_half_transformed_exchange_matrix_s12_kernel(
         def quantize_coef(g):
             coef_mx.append(quantize("coef_%d" % g, coef_staged[g]))
 
-        def sort_phi(j, pair, engine_copy):
+        def sort_phi(j, pair):
             parted = sorted_pool.tile([P, 2, PASSES, 2, P], F32, name="phi_sorted_%d_%d" % (j, pair), tag="sorted")
-            engine_copy(
+            nc.vector.tensor_copy(
                 out=parted[:].rearrange("p i g u c -> p (i g) u c"),
                 in_=phi_raw[(j, pair)][:].bitcast(F32).rearrange("p i (g c u) -> p (i g) u c", g=PASSES, u=2),
             )
@@ -298,31 +333,30 @@ def tile_half_transformed_exchange_matrix_s12_kernel(
             nc.sync.dma_start(out=out[m * P : (m + 1) * P, c0 : c0 + width], in_=result[:])
 
         sort_prim(0)
-        chi_half(0, 0)
+        chi_narrow(0)
         make_factor_rows()
-        sort_prim(1)
-        chi_half(0, 1)
-        quantize_chi(0, 0)
-        sort_phi(0, 0, nc.vector.tensor_copy)
-        sort_phi(0, 1, nc.vector.tensor_copy)
-        chi_half(1, 0)
         stage_coef(0)
+        chi_wide(0)
+        sort_prim(1)
+        quantize_coef(0)
+        sort_phi(0, 0)
+        chi_narrow(1)
+        sort_phi(0, 1)
         stage_coef(1)
         sort_prim(2)
         turn_phi(0)
         turn_factor()
-        quantize_coef(0)
         quantize_coef(1)
-        chi_half(2, 0)
-        sort_phi(1, 0, nc.vector.tensor_copy)
-        sort_phi(1, 1, nc.vector.tensor_copy)
+        quantize_chi(0, 0)
+        chi_narrow(2)
+        sort_phi(1, 0)
+        sort_phi(1, 1)
         quantize_phi(0)
         sort_prim(3)
 
         waiting = [(quantize_chi, (j, 0)) for j in range(1, GROUPS)]
         waiting.extend([(quantize_v, (j,)) for j in range(GROUPS)])
         waiting.extend([(quantize_chi, (j, 1)) for j in range(GROUPS)])
-        chi_to_make = [(GROUPS - 1, 0)] + [(j, 1) for j in range(1, GROUPS)]
 
         def catch_up(count):
             for job, args in waiting[0:count]:
@@ -332,16 +366,23 @@ def tile_half_transformed_exchange_matrix_s12_kernel(
         for j in range(GROUPS):
             if j + 1 < GROUPS:
                 turn_phi(j + 1)
+            if j > 0:
+                join_chi(j - 1, nc.scalar.copy)
             if j + 2 < GROUPS:
-                sort_phi(j + 2, 1, nc.scalar.copy)
-                sort_phi(j + 2, 0, nc.vector.tensor_copy)
+                sort_phi(j + 2, 0)
+                sort_phi(j + 2, 1)
             else:
                 catch_up(CATCH_UP)
             psi_group(j)
             if j + 1 < GROUPS:
                 quantize_phi(j + 1)
-            chi_half(*chi_to_make[j])
-        catch_up(len(waiting))
+            if j == 0:
+                chi_narrow(GROUPS - 1)
+            else:
+                chi_wide(j)
+        catch_up(len(waiting) - 2)
+        join_chi(GROUPS - 1, nc.vector.tensor_copy)
+        catch_up(2)
 
         last = BA // P - 1
         for m in range(last):

@@ -29,7 +29,6 @@ BANK = 512
 BANKS = 8
 STAGED = SLOTS * 512
 CATCH_UP = 3
-WARM_PASSES = 20
 
 
 def tile_half_transformed_exchange_matrix_s12_kernel(
@@ -64,25 +63,6 @@ def tile_half_transformed_exchange_matrix_s12_kernel(
         factor_rows = keep.tile([P, SLOTS, P], F32, name="factor_rows")
         nc.gpsimd.memset(prim_rows_first[:], 0)
         nc.vector.memset(con_scale_tile[:].rearrange("p g n -> p (g n)").bitcast(I32), 0)
-
-        ones = keep.tile([P, 512], BF16, name="ones", align_bytes=64)
-        ones_codes = keep.tile([P, P], U32, name="ones_codes", align_bytes=64)
-        ones_scales = keep.tile([P, P], U8, name="ones_scales", align_bytes=64)
-        nc.gpsimd.memset(ones[:], 1.0)
-        nc.vector.quantize_mx(out=ones_codes[:].bitcast(FP8X4), scales=ones_scales[:], in_=ones[:])
-        warm_bank = next_bank()
-        for n in range(WARM_PASSES):
-            c0 = (n % SLOTS) * P
-            nc.tensor.matmul_mx(
-                out=warm_bank[:, c0 : c0 + P],
-                lhsT=ones_codes[:].bitcast(FP8X4),
-                lhsT_scale=ones_scales[:],
-                rhs=ones_codes[:].bitcast(FP8X4),
-                rhs_scale=ones_scales[:],
-                start=True,
-                stop=True,
-            )
-
         nc.vector.memset(factor_rows[:], 0.0)
         nc.vector.memset(prim_rows_rest[:], 0)
 

from contextlib import ExitStack

import concourse.mybir as mybir
from concourse.masks import make_identity

G, KA, KB, BA, BB = 2048, 1024, 1024, 1024, 512
FLOPS = 2 * (G * KA * BA + G * KB * BB + BA * BB * G)

F32 = mybir.dt.float32
BF16 = mybir.dt.bfloat16
I32 = mybir.dt.int32
U32 = mybir.dt.uint32
U8 = mybir.dt.uint8
FP8X4 = mybir.dt.float8_e4m3fn_x4
FP4X4 = mybir.dt.float4_e2m1fn_x4
ALU = mybir.AluOpType
ACT = mybir.ActivationFunctionType

P = 128
SLOTS = 4
K_PASS = P * SLOTS
GROUPS = G // K_PASS
PASSES = KA // K_PASS
RUN = 8
HALF = BA // 2
WIDE = 256
PAIR = 2 * P
BANK = 512
BANKS = 8
STAGED = SLOTS * 512
CATCH_UP = 3


def tile_half_transformed_exchange_matrix_s12_kernel(
    tc, prim_words, prim_scales, con_words, con_scales, phi, coef, w, rho, out
):
    nc = tc.nc
    with ExitStack() as ctx:
        keep = ctx.enter_context(tc.tile_pool(name="keep", bufs=1))
        stage = ctx.enter_context(tc.tile_pool(name="stage", bufs=4))
        sorted_pool = ctx.enter_context(tc.tile_pool(name="sorted_pool", bufs=4))
        paired_pool = ctx.enter_context(tc.tile_pool(name="paired_pool", bufs=2))
        results = ctx.enter_context(tc.tile_pool(name="results", bufs=4))
        psum = ctx.enter_context(tc.psum_pool(name="psum", bufs=1))
        ctx.enter_context(tc.manual_schedule())

        banks_taken = []

        def next_bank():
            n = len(banks_taken)
            banks_taken.append(n)
            return psum.tile([P, BANK], F32, name="bank_%d" % n, tag="bank%d" % (n % BANKS))

        def quantize(label, staged):
            codes = keep.tile([P, 512], U32, name=label + "_codes", align_bytes=64)
            scales = keep.tile([P, 512], U8, name=label + "_scales", align_bytes=64)
            nc.vector.quantize_mx(out=codes[:].bitcast(FP8X4), scales=scales[:], in_=staged[:])
            return codes, scales

        con_scale_tile = keep.tile([P, PASSES, BA], U8, name="con_scale_tile", align_bytes=64)
        prim_rows_first = keep.tile([P, PASSES, 128], I32, name="prim_rows_first")
        prim_rows_rest = keep.tile([P, PASSES, 384], I32, name="prim_rows_rest")
        factor_rows = keep.tile([P, SLOTS, P], F32, name="factor_rows")
        nc.gpsimd.memset(prim_rows_first[:], 0)
        nc.vector.memset(con_scale_tile[:].rearrange("p g n -> p (g n)").bitcast(I32), 0)
        nc.vector.memset(factor_rows[:], 0.0)
        nc.vector.memset(prim_rows_rest[:], 0)

        ident = keep.tile([P, P], F32, name="ident")
        make_identity(nc, ident[:])

        con_src = con_words.bitcast(I32).rearrange("g p x -> p g x")
        prim_src = prim_words.bitcast(I32).rearrange("g p x -> p g x")
        con_scale_src = con_scales.bitcast(I32).rearrange("g (q r) x -> r q g x", r=4)
        prim_scale_src = prim_scales.bitcast(I32).rearrange("g (q r) x -> r q g x", r=4)

        con_codes = []
        prim_raw = []
        phi_raw = {}
        coef_raw = []

        def load_con(h, queue):
            half = keep.tile([P, PASSES, 2 * HALF], U8, name="con_codes_%d" % h, align_bytes=64)
            queue.dma_start(out=half[:].bitcast(I32), in_=con_src[:, :, 256 * h : 256 * (h + 1)])
            con_codes.append(half)

        def load_prim(j, queue):
            raw = keep.tile([P, PASSES, 256], I32, name="prim_raw_%d" % j)
            queue.dma_start(out=raw[:], in_=prim_src[:, :, 256 * j : 256 * (j + 1)])
            prim_raw.append(raw)

        def load_scale_rows(dst, src):
            for r in range(4):
                nc.sync.dma_start(out=dst[r:P:32, :, :], in_=src[r])

        def load_phi(j):
            for pair in range(2):
                raw = keep.tile([P, 2, KB], BF16, name="phi_raw_%d_%d" % (j, pair))
                row0 = j * K_PASS + pair * PAIR
                nc.sync.dma_start(out=raw[:], in_=phi[row0 : row0 + PAIR, :].rearrange("(i c) k -> c i k", i=2))
                phi_raw[(j, pair)] = raw

        def load_coef(g):
            raw = keep.tile([P, SLOTS, BB], BF16, name="coef_raw_%d" % g)
            rows = coef[g * K_PASS : (g + 1) * K_PASS, :]
            nc.sync.dma_start(out=raw[:], in_=rows.rearrange("(p t) n -> p t n", t=SLOTS))
            coef_raw.append(raw)

        rho_rows = keep.tile([GROUPS, K_PASS], BF16, name="rho_rows")
        w_rows = keep.tile([GROUPS, K_PASS], BF16, name="w_rows")
        nc.sync.dma_start(out=rho_rows[:], in_=rho.rearrange("(j c) -> j c", j=GROUPS))
        load_scale_rows(prim_rows_first, prim_scale_src[:, :, :, 0:128])
        load_prim(0, nc.scalar)
        load_con(0, nc.scalar)
        load_scale_rows(con_scale_tile[:].bitcast(I32), con_scale_src)
        nc.sync.dma_start(out=w_rows[:], in_=w.rearrange("(j c) -> j c", j=GROUPS))
        load_coef(0)
        load_con(1, nc.sync)
        load_prim(1, nc.sync)
        load_scale_rows(prim_rows_rest, prim_scale_src[:, :, :, 128:512])
        load_phi(0)
        load_coef(1)
        for j in range(1, GROUPS):
            if j + 1 < GROUPS:
                load_prim(j + 1, nc.sync)
            load_phi(j)

        prim_sorted = []

        def sort_prim(j):
            codes = keep.tile([P, PASSES, 2 * K_PASS], U8, name="prim_codes_%d" % j, align_bytes=64)
            nc.vector.tensor_copy(
                out=codes[:].bitcast(I32).rearrange("p g (t q x) -> p g t q x", t=SLOTS, x=RUN // 2),
                in_=prim_raw[j][:].rearrange("p g (q t x) -> p g t q x", t=SLOTS, x=RUN // 2),
            )
            rows = prim_rows_first[:] if j == 0 else prim_rows_rest[:, :, (j - 1) * 128 : j * 128]
            scales = keep.tile([P, PASSES, K_PASS], U8, name="prim_scales_%d" % j, align_bytes=64)
            nc.vector.tensor_copy(
                out=scales[:].bitcast(I32).rearrange("p g (t q x) -> p g t q x", t=SLOTS, x=RUN // 4),
                in_=rows.rearrange("p g (q t x) -> p g t q x", t=SLOTS, x=RUN // 4),
            )
            prim_sorted.append((codes, scales))

        log_rho = keep.tile([GROUPS, K_PASS], F32, name="log_rho")
        root = keep.tile([GROUPS, K_PASS], F32, name="root")
        factor = keep.tile([P, GROUPS, SLOTS], F32, name="factor")
        nc.scalar.activation(out=log_rho[:], in_=rho_rows[:], func=ACT.Ln)
        nc.scalar.activation(out=root[:], in_=log_rho[:], func=ACT.Exp, scale=1.0 / 3.0)

        def make_factor_rows():
            nc.vector.tensor_tensor(
                out=factor_rows[0:GROUPS, :, :].rearrange("p t (q r) -> p q t r", r=RUN),
                in0=root[:].rearrange("p (q t r) -> p q t r", t=SLOTS, r=RUN),
                in1=w_rows[:].rearrange("p (q t r) -> p q t r", t=SLOTS, r=RUN),
                op=ALU.mult,
            )

        def turn_factor():
            bank = next_bank()
            for t in range(SLOTS):
                nc.tensor.transpose(bank[:, t * P : (t + 1) * P], factor_rows[:, t, :], ident[:])
            nc.scalar.copy(out=factor[:], in_=bank[:].rearrange("p (t j) -> p j t", t=SLOTS)[:, 0:GROUPS, :])

        chi_staged = {}
        chi_paired = {}
        chi_mx = {}
        coef_staged = []
        coef_mx = []
        phi_sorted = {}
        phi_staged = {}
        phi_mx = {}
        v_staged = {}
        v_mx = {}

        def chi_narrow(j):
            codes, scales = prim_sorted[j]
            staged = keep.tile([P, STAGED], BF16, name="chi_staged_%d_0" % j, align_bytes=64)
            for n in range(HALF // P):
                bank = next_bank()
                for t in range(SLOTS):
                    for g in range(PASSES):
                        nc.tensor.matmul_mx(
                            out=bank[:, t * P : (t + 1) * P],
                            lhsT=codes[:, g, 2 * t * P : 2 * (t + 1) * P].bitcast(FP4X4),
                            lhsT_scale=scales[:, g, t * P : (t + 1) * P],
                            rhs=con_codes[0][:, g, 2 * n * P : 2 * (n + 1) * P].bitcast(FP4X4),
                            rhs_scale=con_scale_tile[:, g, n * P : (n + 1) * P],
                            start=(g == 0),
                            stop=(g == PASSES - 1),
                        )
                nc.scalar.copy(
                    out=staged[:, n * BANK : (n + 1) * BANK].rearrange("p (c t) -> p c t", t=SLOTS),
                    in_=bank[:].rearrange("p (t c) -> p c t", t=SLOTS),
                )
            chi_staged[(j, 0)] = staged

        def chi_wide(j):
            codes, scales = prim_sorted[j]
            paired = paired_pool.tile([P, HALF // WIDE, 2, BANK], BF16, name="chi_paired_%d" % j, tag="paired")
            for n in range(HALF // WIDE):
                col0 = HALF + n * WIDE
                for u in range(2):
                    bank = next_bank()
                    for e in range(2):
                        t = 2 * u + e
                        for g in range(PASSES):
                            nc.tensor.matmul_mx(
                                out=bank[:, e * WIDE : (e + 1) * WIDE],
                                lhsT=codes[:, g, 2 * t * P : 2 * (t + 1) * P].bitcast(FP4X4),
                                lhsT_scale=scales[:, g, t * P : (t + 1) * P],
                                rhs=con_codes[1][:, g, 2 * n * WIDE : 2 * (n + 1) * WIDE].bitcast(FP4X4),
                                rhs_scale=con_scale_tile[:, g, col0 : col0 + WIDE],
                                start=(g == 0),
                                stop=(g == PASSES - 1),
                            )
                    nc.scalar.copy(
                        out=paired[:, n, u, :].rearrange("p (c e) -> p c e", e=2),
                        in_=bank[:].rearrange("p (e c) -> p c e", e=2),
                    )
            chi_paired[j] = paired

        def join_chi(j, engine_copy):
            staged = keep.tile([P, STAGED], BF16, name="chi_staged_%d_1" % j, align_bytes=64)
            engine_copy(
                out=staged[:].bitcast(F32).rearrange("p (n c u) -> p n c u", n=HALF // WIDE, u=2),
                in_=chi_paired[j][:].bitcast(F32).rearrange("p n u c -> p n c u"),
            )
            chi_staged[(j, 1)] = staged

        def quantize_chi(j, h):
            chi_mx[(j, h)] = quantize("chi_%d_%d" % (j, h), chi_staged[(j, h)])

        def stage_coef(g):
            staged = stage.tile([P, STAGED], BF16, name="coef_staged_%d" % g, tag="staged", align_bytes=64)
            nc.vector.tensor_copy(
                out=staged[:].rearrange("p (c i t) -> p c t i", i=4, t=SLOTS),
                in_=coef_raw[g][:].rearrange("p t (c i) -> p c t i", i=4),
            )
            coef_staged.append(staged)

        def quantize_coef(g):
            coef_mx.append(quantize("coef_%d" % g, coef_staged[g]))

        def sort_phi(j, pair):
            parted = sorted_pool.tile([P, 2, PASSES, 2, P], F32, name="phi_sorted_%d_%d" % (j, pair), tag="sorted")
            nc.vector.tensor_copy(
                out=parted[:].rearrange("p i g u c -> p (i g) u c"),
                in_=phi_raw[(j, pair)][:].bitcast(F32).rearrange("p i (g c u) -> p (i g) u c", g=PASSES, u=2),
            )
            phi_sorted[(j, pair)] = parted

        def turn_phi(j):
            for g in range(PASSES):
                staged = stage.tile([P, STAGED], BF16, name="phi_staged_%d_%d" % (j, g), tag="staged", align_bytes=64)
                words = staged[:].bitcast(F32).rearrange("p (t q r u) -> p q t r u", t=SLOTS, r=RUN, u=2)
                for pair in range(2):
                    bank = next_bank()
                    for u in range(2):
                        for i in range(2):
                            c0 = (2 * u + i) * P
                            nc.tensor.transpose(bank[:, c0 : c0 + P], phi_sorted[(j, pair)][:, i, g, u, :], ident[:])
                    nc.scalar.copy(
                        out=words[:, 8 * pair : 8 * (pair + 1), :, :, :],
                        in_=bank[:].rearrange("p (u q t r) -> p q t r u", u=2, t=SLOTS, r=RUN),
                    )
                phi_staged[(j, g)] = staged

        def quantize_phi(j):
            for g in range(PASSES):
                phi_mx[(j, g)] = quantize("phi_%d_%d" % (j, g), phi_staged[(j, g)])

        def psi_group(j):
            staged = keep.tile([P, STAGED], BF16, name="v_staged_%d" % j, align_bytes=64)
            for n in range(BB // P):
                bank = next_bank()
                for t in range(SLOTS):
                    for g in range(PASSES):
                        nc.tensor.matmul_mx(
                            out=bank[:, t * P : (t + 1) * P],
                            lhsT=phi_mx[(j, g)][0][:, t * P : (t + 1) * P].bitcast(FP8X4),
                            lhsT_scale=phi_mx[(j, g)][1][:, t * P : (t + 1) * P],
                            rhs=coef_mx[g][0][:, n * P : (n + 1) * P].bitcast(FP8X4),
                            rhs_scale=coef_mx[g][1][:, n * P : (n + 1) * P],
                            start=(g == 0),
                            stop=(g == PASSES - 1),
                        )
                nc.vector.tensor_tensor(
                    out=staged[:, n * BANK : (n + 1) * BANK].rearrange("p (c t) -> p c t", t=SLOTS),
                    in0=bank[:].rearrange("p (t c) -> p c t", t=SLOTS),
                    in1=factor[:, j : j + 1, :].to_broadcast([P, P, SLOTS]),
                    op=ALU.mult,
                )
            v_staged[j] = staged

        def quantize_v(j):
            v_mx[j] = quantize("v_%d" % j, v_staged[j])

        def out_tile(m, c0, width, engine_copy):
            h, n = divmod(m, HALF // P)
            bank = next_bank()
            for j in range(GROUPS):
                nc.tensor.matmul_mx(
                    out=bank[:, 0:width],
                    lhsT=chi_mx[(j, h)][0][:, n * P : (n + 1) * P].bitcast(FP8X4),
                    lhsT_scale=chi_mx[(j, h)][1][:, n * P : (n + 1) * P],
                    rhs=v_mx[j][0][:, c0 : c0 + width].bitcast(FP8X4),
                    rhs_scale=v_mx[j][1][:, c0 : c0 + width],
                    start=(j == 0),
                    stop=(j == GROUPS - 1),
                )
            result = results.tile([P, width], F32, name="result_%d_%d" % (m, c0), tag="result")
            engine_copy(out=result[:], in_=bank[:, 0:width])
            nc.sync.dma_start(out=out[m * P : (m + 1) * P, c0 : c0 + width], in_=result[:])

        sort_prim(0)
        chi_narrow(0)
        make_factor_rows()
        stage_coef(0)
        chi_wide(0)
        sort_prim(1)
        quantize_coef(0)
        sort_phi(0, 0)
        chi_narrow(1)
        sort_phi(0, 1)
        stage_coef(1)
        sort_prim(2)
        turn_phi(0)
        turn_factor()
        quantize_coef(1)
        quantize_chi(0, 0)
        chi_narrow(2)
        sort_phi(1, 0)
        sort_phi(1, 1)
        quantize_phi(0)
        sort_prim(3)

        waiting = [(quantize_chi, (j, 0)) for j in range(1, GROUPS)]
        waiting.extend([(quantize_v, (j,)) for j in range(GROUPS)])
        waiting.extend([(quantize_chi, (j, 1)) for j in range(GROUPS)])

        def catch_up(count):
            for job, args in waiting[0:count]:
                waiting.remove((job, args))
                job(*args)

        for j in range(GROUPS):
            if j + 1 < GROUPS:
                turn_phi(j + 1)
            if j > 0:
                join_chi(j - 1, nc.scalar.copy)
            if j + 2 < GROUPS:
                sort_phi(j + 2, 0)
                sort_phi(j + 2, 1)
            else:
                catch_up(CATCH_UP)
            psi_group(j)
            if j + 1 < GROUPS:
                quantize_phi(j + 1)
            if j == 0:
                chi_narrow(GROUPS - 1)
            else:
                chi_wide(j)
        catch_up(len(waiting) - 2)
        join_chi(GROUPS - 1, nc.vector.tensor_copy)
        catch_up(2)

        last = BA // P - 1
        for m in range(last):
            out_tile(m, 0, BB, nc.scalar.copy)
        out_tile(last, 0, BB // 2, nc.vector.tensor_copy)
        out_tile(last, BB // 2, BB // 2, nc.scalar.copy)
